import numpy as np
import ml_dtypes


def mxq(x, axis, fmt="e4m3"):
    dtype, down = {"e4m3": (ml_dtypes.float8_e4m3fn, 7), "e5m2": (ml_dtypes.float8_e5m2, 14)}[fmt]
    v = np.moveaxis(np.asarray(x, np.float32).astype(ml_dtypes.bfloat16).astype(np.float64), axis, -1)
    blocks = v.reshape(v.shape[:-1] + (-1, 32))
    amax = np.abs(blocks).max(-1, keepdims=True)
    byte = np.maximum(np.where(amax > 0, np.frexp(amax)[1] - 1 + 127, 0) - down, 1)
    scale = np.exp2(byte - 127.0)
    codes = (blocks / scale).astype(np.float32).astype(dtype).astype(np.float64)
    return np.moveaxis((codes * scale).reshape(v.shape), -1, axis)


WIDE = False


def mx_kscale(k):
    if not WIDE:
        return np.ones(k)
    levels = np.array([10, -10, 5, -5, 0])
    if k % 512:
        return np.exp2(np.random.permutation(np.resize(levels, k // 32))).repeat(32)
    a = np.empty((k // 512, 16))
    for p in range(k // 512):
        a[p, :8] = np.random.permutation(np.resize(levels, 8))
        for g in range(8):
            far = levels[np.abs(levels - a[p, g]) >= 10]
            a[p, g + 8] = far[np.random.randint(len(far))]
    return np.exp2(a.ravel()).repeat(32)


BF16 = ml_dtypes.bfloat16


def bf(x):
    return np.asarray(x, np.float32).astype(BF16)


def f64(x):
    return np.asarray(x).astype(np.float64)


E2M1 = np.array([0.0, 0.5, 1.0, 1.5, 2.0, 3.0, 4.0, 6.0, -0.0, -0.5, -1.0, -1.5, -2.0, -3.0, -4.0, -6.0])


def pack_weight(w, fmt):
    k, n = w.shape
    w = f64(bf(w)).reshape(k // 32, 32, n)
    amax = np.abs(w).max(1)
    if fmt == "e4m3":
        byte = np.frexp(amax)[1] - 1 + 127 - 7
    else:
        mant, ex = np.frexp(amax / 6.0)
        byte = np.where(mant > 0.5, ex, ex - 1) + 127
    byte = np.clip(np.where(amax > 0, byte, 1), 1, 254)
    scaled = (w * np.exp2(127.0 - byte)[:, None, :]).reshape(k, n).astype(np.float32)
    by_word = np.ascontiguousarray(scaled.reshape(k // 512, 128, 4, n).transpose(0, 1, 3, 2))
    if fmt == "e4m3":
        words = by_word.astype(ml_dtypes.float8_e4m3fn).view(np.uint8)
    else:
        c = by_word.astype(ml_dtypes.float4_e2m1fn).view(np.uint8) & 0xF
        words = c[..., 0::2] | (c[..., 1::2] << 4)
    return np.ascontiguousarray(words), np.ascontiguousarray(byte.astype(np.uint8).reshape(k // 512, 16, n))


def unpack_weight(words, scales, fmt):
    g, p, n, _ = words.shape
    if fmt == "e4m3":
        vals = np.ascontiguousarray(words).view(ml_dtypes.float8_e4m3fn).astype(np.float64)
    else:
        nib = np.empty((g, p, n, 4), np.uint8)
        nib[..., 0::2] = words & 0xF
        nib[..., 1::2] = words >> 4
        vals = E2M1[nib]
    vals = vals * np.repeat(np.exp2(scales.astype(np.float64) - 127.0), 8, axis=1)[..., None]
    return vals.transpose(0, 1, 3, 2).reshape(g * 512, n)
def pack4(w):
    words, scales = pack_weight(w, "e2m1")
    return words.reshape(words.shape[0], 128, -1), scales


def unpack4(words, scales):
    return unpack_weight(words.reshape(words.shape[0], 128, -1, 2), scales, "e2m1")


G, K, R, Q, N, P = 4, 1024, 512, 1024, 512, 16


def setup_inputs():
    s = mx_kscale(K)
    t = mx_kscale(Q)
    so = np.exp(0.5 * np.random.standard_normal((G, R // P))).repeat(P, axis=1)
    sc = np.exp(0.5 * np.random.standard_normal((G, Q // P))).repeat(P, axis=1)
    lo = np.random.standard_normal((G, K, R)) * so[:, None, :]
    lc = np.random.standard_normal((G, K, Q)) / np.sqrt(K) * sc[:, None, :]
    fo = np.sqrt((lo ** 2).sum(axis=1).reshape(G, R // P, P).sum(axis=2))
    fc = np.sqrt((lc ** 2).sum(axis=1).reshape(G, Q // P, P).sum(axis=2))
    o_inv = (np.sqrt(K * P) / fo).repeat(P, axis=1)
    c_inv = (np.sqrt(P) / fc).repeat(P, axis=1)
    om = np.random.standard_normal((G, Q, N)) / np.sqrt(Q)
    lc_words, lc_scales = pack4((lc / s[:, None]).reshape(G * K, Q))
    om_words, om_scales = pack4((om / t[:, None]).reshape(G * Q, N))
    return {"lo": bf(lo * s[:, None]),
            "lc_words": lc_words, "lc_scales": lc_scales,
            "o_inv": bf(o_inv), "c_inv": bf(c_inv * t),
            "om_words": om_words, "om_scales": om_scales}


def reference(lo, lc_words, lc_scales, o_inv, c_inv, om_words, om_scales):
    lc = unpack4(lc_words, lc_scales).reshape(G, K, Q)
    om = unpack4(om_words, om_scales).reshape(G, Q, N)
    h = mxq(f64(lo), 1, "e4m3").swapaxes(1, 2) @ lc
    h = h * f64(c_inv)[:, None, :]
    y = mxq(h, 2, "e4m3") @ om
    return y * f64(o_inv)[:, :, None]

@@ -1,0 +1,234 @@
+from contextlib import ExitStack
+
+import concourse.mybir as mybir
+from concourse.masks import make_identity
+
+G, K, R, Q, N = 4, 1024, 512, 1024, 512
+FLOPS = 2 * G * (K * R * Q + R * Q * N)
+
+F32 = mybir.dt.float32
+BF16 = mybir.dt.bfloat16
+I32 = mybir.dt.int32
+U32 = mybir.dt.uint32
+U8 = mybir.dt.uint8
+FP8X4 = mybir.dt.float8_e4m3fn_x4
+FP4X4 = mybir.dt.float4_e2m1fn_x4
+COPY = mybir.ActivationFunctionType.Copy
+MULT = mybir.AluOpType.mult
+
+P = 128
+PACK = 4
+K_PASS = P * PACK
+PASSES = 2
+BANK = 512
+TILES = G * R // P
+PAIRS = TILES // 2
+HALF = R // 2
+
+
+def tile_scaled_hankel_sketch_s14_kernel(tc, lo, lc_words, lc_scales, o_inv, c_inv, om_words, om_scales, out):
+    nc = tc.nc
+    with ExitStack() as ctx:
+        keep = ctx.enter_context(tc.tile_pool(name="keep", bufs=1))
+        flow = ctx.enter_context(tc.tile_pool(name="flow", bufs=6))
+        psum = ctx.enter_context(tc.psum_pool(name="psum", bufs=1))
+        ctx.enter_context(tc.manual_schedule())
+
+        lc_w32, lc_s32 = lc_words.bitcast(I32), lc_scales.bitcast(I32)
+        om_w32, om_s32 = om_words.bitcast(I32), om_scales.bitcast(I32)
+
+        def bank(tag, shape):
+            return psum.tile(shape, F32, tag=tag, name=tag)
+
+        def scale_plane(name, passes, width):
+            plane = keep.tile([P, passes, width], U8, name=name, align_bytes=64)
+            nc.vector.memset(plane[:].bitcast(I32), 0)
+            return plane
+
+        def load_scales(plane, rows):
+            for quad in range(4):
+                nc.sync.dma_start(
+                    out=plane[32 * quad : 32 * quad + 4].bitcast(I32),
+                    in_=rows[:, 4 * quad : 4 * quad + 4, :].rearrange("g r n -> r g n"),
+                )
+
+        def load_words(name, rows):
+            passes, unused, words = rows.shape
+            codes = keep.tile([P, passes, 4 * words], U8, name=name, align_bytes=64)
+            nc.sync.dma_start(out=codes[:].bitcast(I32), in_=rows.rearrange("g p n -> p g n"))
+            return codes
+
+        def load_lo(j, g, c0, c1):
+            raw = keep.tile([P, PACK, c1 - c0], BF16, name="lo_%d_%d_%d" % (j, g, c0), align_bytes=64)
+            rows = lo[j, g * K_PASS : (g + 1) * K_PASS, c0:c1]
+            nc.sync.dma_start(out=raw[:], in_=rows.rearrange("(p t) r -> p t r", t=PACK))
+            return raw
+
+        c_scale0 = scale_plane("c_scale0", PASSES, Q)
+        e_scale = scale_plane("e_scale", G * PASSES, N)
+        c_scale1 = scale_plane("c_scale1", (G - 1) * PASSES, Q)
+        ident = keep.tile([P, P], F32, name="ident")
+        make_identity(nc, ident[:])
+        o_pad = keep.tile([P, P], F32, name="o_pad")
+        nc.gpsimd.memset(o_pad[:], 0.0)
+
+        c_quads = keep.tile([P, G * PASSES, PACK], BF16, name="c_quads")
+        nc.sync.dma_start(out=c_quads[:], in_=c_inv.rearrange("j (g p t) -> p (j g) t", p=P, t=PACK))
+        o_rows = keep.tile([TILES, P], BF16, name="o_rows")
+        nc.sync.dma_start(out=o_rows[:], in_=o_inv.rearrange("j (i p) -> (j i) p", p=P))
+
+        raw_lo = {}
+        c_words = {}
+        e_words = {}
+
+        def load_lo_half(h):
+            for g in range(PASSES):
+                raw = load_lo(0, g, h * HALF, (h + 1) * HALF)
+                for i in range(2):
+                    raw_lo[(2 * h + i, g)] = raw[:, :, i * P : (i + 1) * P]
+
+        load_lo_half(0)
+        load_scales(c_scale0, lc_s32[0:PASSES])
+        for h in range(2):
+            codes = load_words("c_words_0_%d" % h, lc_w32[0:PASSES, :, h * 256 : (h + 1) * 256])
+            for g in range(PASSES):
+                c_words[(0, g, h)] = codes[:, g, :]
+        load_lo_half(1)
+        e_words[0] = load_words("e_words_0", om_w32[0:PASSES])
+        load_scales(e_scale, om_s32)
+        load_scales(c_scale1, lc_s32[PASSES:])
+        for j in range(1, G):
+            for g in range(PASSES):
+                raw = load_lo(j, g, 0, R)
+                for i in range(4):
+                    raw_lo[(4 * j + i, g)] = raw[:, :, i * P : (i + 1) * P]
+            codes = load_words("c_words_%d" % j, lc_w32[PASSES * j : PASSES * (j + 1)])
+            for g in range(PASSES):
+                for h in range(2):
+                    c_words[(j, g, h)] = codes[:, g, h * 1024 : (h + 1) * 1024]
+            e_words[j] = load_words("e_words_%d" % j, om_w32[PASSES * j : PASSES * (j + 1)])
+
+        def c_scales(j, g, h):
+            plane = c_scale0[:, g, :] if j == 0 else c_scale1[:, PASSES * (j - 1) + g, :]
+            return plane[:, h * BANK : (h + 1) * BANK]
+
+        grouped, lo_q, hs, ht, h_q = {}, {}, {}, {}, {}
+
+        def interleave(u, g, copy):
+            if u not in grouped:
+                grouped[u] = flow.tile([P, PASSES, P, PACK], BF16, tag="grouped", name="grouped", align_bytes=64)
+            copy(
+                out=grouped[u][:, g].rearrange("p (c i) t -> p c t i", i=4),
+                in_=raw_lo[(u, g)].rearrange("p t (c i) -> p c t i", i=4),
+            )
+
+        def quantize(values, tag):
+            codes = flow.tile([P, PASSES * P], U32, tag=tag + "_codes", name=tag + "_codes", align_bytes=64)
+            scales = flow.tile([P, PASSES * P], U8, tag=tag + "_scales", name=tag + "_scales", align_bytes=64)
+            nc.vector.quantize_mx(out=codes[:].bitcast(FP8X4), scales=scales[:], in_=values)
+            return codes, scales
+
+        def quantize_lo(u):
+            lo_q[u] = quantize(grouped[u][:].rearrange("p g r t -> p (g r t)"), "lo")
+
+        def quantize_h(u):
+            h_q[u] = quantize(ht[u][:].rearrange("p g r u -> p (g r u)").bitcast(BF16), "h")
+
+        def product(acc, stationary, moving, moving_scales):
+            codes, scales = stationary
+            for g in range(PASSES):
+                nc.tensor.matmul_mx(
+                    out=acc[:],
+                    lhsT=codes[:, g * P : (g + 1) * P].bitcast(FP8X4),
+                    lhsT_scale=scales[:, g * P : (g + 1) * P],
+                    rhs=moving[g].bitcast(FP4X4),
+                    rhs_scale=moving_scales[g],
+                    start=(g == 0),
+                    stop=(g == PASSES - 1),
+                )
+
+        def hankel(u):
+            j = u // 4
+            hs[u] = flow.tile([P, PASSES, 2, P, 2], BF16, tag="hs", name="hs")
+            for h in range(2):
+                acc = bank("h%d" % (2 * (u % 2) + h), [P, BANK])
+                product(acc, lo_q[u], [c_words[(j, g, h)] for g in range(PASSES)], [c_scales(j, g, h) for g in range(PASSES)])
+                nc.vector.tensor_tensor(
+                    out=hs[u][:, h],
+                    in0=acc[:].rearrange("r (p u e) -> r u p e", u=2, e=2),
+                    in1=c_rows[j][:, h],
+                    op=MULT,
+                )
+
+        def turn(u, copy):
+            words = hs[u][:].rearrange("r g u p e -> r (g u p e)").bitcast(F32)
+            turned = bank("t%d" % (u % 2), [P, 2 * PASSES, P])
+            for i in range(2 * PASSES):
+                nc.tensor.transpose(turned[:, i, :], words[:, i * P : (i + 1) * P], ident[:])
+            ht[u] = flow.tile([P, PASSES, P, 2], F32, tag="ht", name="ht", align_bytes=64)
+            copy(out=ht[u][:], in_=turned[:].rearrange("p (g u) r -> p g r u", u=2))
+
+        def sketch(u, on_vector):
+            j, i = divmod(u, 4)
+            acc = bank("y%d" % (u % 2), [P, BANK])
+            product(acc, h_q[u], [e_words[j][:, g, :] for g in range(PASSES)], [e_scale[:, PASSES * j + g, :] for g in range(PASSES)])
+            result = flow.tile([P, N], F32, tag="result", name="result")
+            if on_vector:
+                nc.vector.tensor_scalar(out=result[:], in0=acc[:], scalar1=o_cols[:, u : u + 1], scalar2=None, op0=MULT)
+            else:
+                nc.scalar.activation(out=result[:], in_=acc[:], func=COPY, scale=o_cols[:, u : u + 1])
+            nc.sync.dma_start(out=out[j, i * P : (i + 1) * P, :], in_=result[:])
+
+        nc.scalar.activation(out=o_pad[0:TILES, :], in_=o_rows[:], func=COPY)
+        c_pairs = c_quads[:].rearrange("p m t -> p (m t)").bitcast(F32)
+        c_banks = []
+        for j, tag in enumerate(("t0", "t1", "y0", "y1")):
+            spread = bank(tag, [P, 2 * PASSES, P])
+            for i in range(2 * PASSES):
+                m = 2 * PASSES * j + i
+                nc.tensor.transpose(spread[:, i, :], c_pairs[:, m : m + 1].to_broadcast([P, P]), ident[:])
+            c_banks.append(spread)
+        o_bank = bank("h3", [P, P])
+        nc.tensor.transpose(o_bank[:], o_pad[:], ident[:])
+        o_cols = keep.tile([P, TILES], F32, name="o_cols")
+        c_rows = {}
+
+        def fetch_c(j):
+            words = keep.tile([P, 2 * PASSES * P], F32, name="c_rows_%d" % j)
+            nc.scalar.copy(out=words[:], in_=c_banks[j][:].rearrange("r i p -> r (i p)"))
+            c_rows[j] = words[:].bitcast(BF16).rearrange("r (g u p e) -> r g u p e", g=PASSES, u=2, e=2)
+
+        for g in range(PASSES):
+            interleave(0, g, nc.vector.tensor_copy)
+            interleave(1, g, nc.scalar.copy)
+        fetch_c(0)
+        nc.scalar.copy(out=o_cols[:], in_=o_bank[:, 0:TILES])
+        quantize_lo(0)
+        quantize_lo(1)
+        interleave(2, 0, nc.vector.tensor_copy)
+
+        for k in range(PAIRS + 2):
+            if 2 <= k:
+                quantize_h(2 * k - 4)
+                quantize_h(2 * k - 3)
+            if k + 1 < PAIRS:
+                interleave(2 * k + 2, 1, nc.scalar.copy)
+                interleave(2 * k + 3, 0, nc.scalar.copy)
+                interleave(2 * k + 3, 1, nc.scalar.copy)
+            if k == 0:
+                for j in range(1, G):
+                    fetch_c(j)
+            if k < PAIRS:
+                hankel(2 * k)
+                hankel(2 * k + 1)
+            if k + 1 < PAIRS:
+                quantize_lo(2 * k + 2)
+                quantize_lo(2 * k + 3)
+            if k + 2 < PAIRS:
+                interleave(2 * k + 4, 0, nc.vector.tensor_copy)
+            if 1 <= k <= PAIRS:
+                turn(2 * k - 2, nc.scalar.copy)
+                turn(2 * k - 1, nc.vector.tensor_copy if k == PAIRS else nc.scalar.copy)
+            if 2 <= k:
+                sketch(2 * k - 4, False)
+                sketch(2 * k - 3, k == PAIRS + 1)

@@ -23,14 +23,16 @@ PASSES = 2
 BANK = 512
 TILES = G * R // P
 PAIRS = TILES // 2
-HALF = R // 2
+PAIR_COLS = 2 * P
+SCALAR_COLS = 64
+HEAD_SCALAR_COLS = 80
 
 
 def tile_scaled_hankel_sketch_s14_kernel(tc, lo, lc_words, lc_scales, o_inv, c_inv, om_words, om_scales, out):
     nc = tc.nc
     with ExitStack() as ctx:
         keep = ctx.enter_context(tc.tile_pool(name="keep", bufs=1))
-        flow = ctx.enter_context(tc.tile_pool(name="flow", bufs=6))
+        flow = ctx.enter_context(tc.tile_pool(name="flow", bufs=4))
         psum = ctx.enter_context(tc.psum_pool(name="psum", bufs=1))
         ctx.enter_context(tc.manual_schedule())
 
@@ -40,17 +42,23 @@ def tile_scaled_hankel_sketch_s14_kernel(tc, lo, lc_words, lc_scales, o_inv, c_i
         def bank(tag, shape):
             return psum.tile(shape, F32, tag=tag, name=tag)
 
-        def scale_plane(name, passes, width):
-            plane = keep.tile([P, passes, width], U8, name=name, align_bytes=64)
+        def scale_plane(name, j0, j1, width):
+            plane = keep.tile([P, PASSES * (j1 - j0), width], U8, name=name, align_bytes=64)
             nc.vector.memset(plane[:].bitcast(I32), 0)
             return plane
 
-        def load_scales(plane, rows):
+        raw_lo, c_words, c_scales, e_words, e_scales = {}, {}, {}, {}, {}
+
+        def load_scales(plane, rows, j0, j1, found):
+            rows = rows[PASSES * j0 : PASSES * j1]
             for quad in range(4):
                 nc.sync.dma_start(
                     out=plane[32 * quad : 32 * quad + 4].bitcast(I32),
                     in_=rows[:, 4 * quad : 4 * quad + 4, :].rearrange("g r n -> r g n"),
                 )
+            for j in range(j0, j1):
+                for g in range(PASSES):
+                    found[(j, g)] = plane[:, PASSES * (j - j0) + g, :]
 
         def load_words(name, rows):
             passes, unused, words = rows.shape
@@ -58,177 +66,216 @@ def tile_scaled_hankel_sketch_s14_kernel(tc, lo, lc_words, lc_scales, o_inv, c_i
             nc.sync.dma_start(out=codes[:].bitcast(I32), in_=rows.rearrange("g p n -> p g n"))
             return codes
 
-        def load_lo(j, g, c0, c1):
-            raw = keep.tile([P, PACK, c1 - c0], BF16, name="lo_%d_%d_%d" % (j, g, c0), align_bytes=64)
-            rows = lo[j, g * K_PASS : (g + 1) * K_PASS, c0:c1]
+        def load_lo(j, g):
+            raw = keep.tile([P, PACK, R], BF16, name="lo_%d_%d" % (j, g), align_bytes=64)
+            rows = lo[j, g * K_PASS : (g + 1) * K_PASS, :]
             nc.sync.dma_start(out=raw[:], in_=rows.rearrange("(p t) r -> p t r", t=PACK))
-            return raw
+            raw_lo[(j, g)] = raw
 
-        c_scale0 = scale_plane("c_scale0", PASSES, Q)
-        e_scale = scale_plane("e_scale", G * PASSES, N)
-        c_scale1 = scale_plane("c_scale1", (G - 1) * PASSES, Q)
+        def load_c_words(j, h0, h1):
+            codes = load_words("c_words_%d_%d" % (j, h0), lc_w32[PASSES * j : PASSES * (j + 1), :, h0 * 256 : h1 * 256])
+            for g in range(PASSES):
+                for h in range(h0, h1):
+                    c_words[(j, g, h)] = codes[:, g, (h - h0) * 1024 : (h - h0 + 1) * 1024]
+
+        def load_e_words(j0, j1):
+            codes = load_words("e_words_%d" % j0, om_w32[PASSES * j0 : PASSES * j1])
+            for j in range(j0, j1):
+                for g in range(PASSES):
+                    e_words[(j, g)] = codes[:, PASSES * (j - j0) + g, :]
+
+        factors = keep.tile([P, P], F32, name="factors")
+        nc.gpsimd.memset(factors[:], 0.0)
+        c_plane0 = scale_plane("c_plane0", 0, 1, Q)
+        c_plane1 = scale_plane("c_plane1", 1, 2, Q)
+        e_plane0 = scale_plane("e_plane0", 0, 1, N)
+        c_plane2 = scale_plane("c_plane2", 2, G, Q)
+        e_plane1 = scale_plane("e_plane1", 1, G, N)
         ident = keep.tile([P, P], F32, name="ident")
         make_identity(nc, ident[:])
-        o_pad = keep.tile([P, P], F32, name="o_pad")
-        nc.gpsimd.memset(o_pad[:], 0.0)
 
-        c_quads = keep.tile([P, G * PASSES, PACK], BF16, name="c_quads")
-        nc.sync.dma_start(out=c_quads[:], in_=c_inv.rearrange("j (g p t) -> p (j g) t", p=P, t=PACK))
         o_rows = keep.tile([TILES, P], BF16, name="o_rows")
         nc.sync.dma_start(out=o_rows[:], in_=o_inv.rearrange("j (i p) -> (j i) p", p=P))
+        load_lo(0, 0)
+        nc.sync.dma_start(out=factors[TILES : 2 * TILES, :].bitcast(BF16), in_=c_inv.rearrange("j (m w) -> (j m) w", w=2 * P))
+        load_lo(0, 1)
+        load_scales(c_plane0, lc_s32, 0, 1, c_scales)
+        load_c_words(0, 0, 1)
+        load_c_words(0, 1, 2)
+        load_lo(1, 0)
+        load_lo(1, 1)
+        load_scales(c_plane1, lc_s32, 1, 2, c_scales)
+        load_c_words(1, 0, 2)
+        load_scales(e_plane0, om_s32, 0, 1, e_scales)
+        load_e_words(0, 1)
+        load_lo(2, 0)
+        load_lo(2, 1)
+        load_scales(c_plane2, lc_s32, 2, G, c_scales)
+        load_c_words(2, 0, 2)
+        load_scales(e_plane1, om_s32, 1, G, e_scales)
+        load_e_words(1, 2)
+        load_lo(3, 0)
+        load_lo(3, 1)
+        load_c_words(3, 0, 2)
+        load_e_words(2, G)
 
-        raw_lo = {}
-        c_words = {}
-        e_words = {}
+        grouped, lo_q, hs, ht, h_q, y_acc, c_banks, c_rows = {}, {}, {}, {}, {}, {}, {}, {}
 
-        def load_lo_half(h):
-            for g in range(PASSES):
-                raw = load_lo(0, g, h * HALF, (h + 1) * HALF)
-                for i in range(2):
-                    raw_lo[(2 * h + i, g)] = raw[:, :, i * P : (i + 1) * P]
-
-        load_lo_half(0)
-        load_scales(c_scale0, lc_s32[0:PASSES])
-        for h in range(2):
-            codes = load_words("c_words_0_%d" % h, lc_w32[0:PASSES, :, h * 256 : (h + 1) * 256])
-            for g in range(PASSES):
-                c_words[(0, g, h)] = codes[:, g, :]
-        load_lo_half(1)
-        e_words[0] = load_words("e_words_0", om_w32[0:PASSES])
-        load_scales(e_scale, om_s32)
-        load_scales(c_scale1, lc_s32[PASSES:])
-        for j in range(1, G):
-            for g in range(PASSES):
-                raw = load_lo(j, g, 0, R)
-                for i in range(4):
-                    raw_lo[(4 * j + i, g)] = raw[:, :, i * P : (i + 1) * P]
-            codes = load_words("c_words_%d" % j, lc_w32[PASSES * j : PASSES * (j + 1)])
-            for g in range(PASSES):
-                for h in range(2):
-                    c_words[(j, g, h)] = codes[:, g, h * 1024 : (h + 1) * 1024]
-            e_words[j] = load_words("e_words_%d" % j, om_w32[PASSES * j : PASSES * (j + 1)])
-
-        def c_scales(j, g, h):
-            plane = c_scale0[:, g, :] if j == 0 else c_scale1[:, PASSES * (j - 1) + g, :]
-            return plane[:, h * BANK : (h + 1) * BANK]
-
-        grouped, lo_q, hs, ht, h_q = {}, {}, {}, {}, {}
-
-        def interleave(u, g, copy):
-            if u not in grouped:
-                grouped[u] = flow.tile([P, PASSES, P, PACK], BF16, tag="grouped", name="grouped", align_bytes=64)
+        def interleave(k, g, c0, c1, copy):
+            if k not in grouped:
+                grouped[k] = flow.tile([P, PASSES, PAIR_COLS, PACK], BF16, tag="grouped", name="grouped", align_bytes=64)
+            first = (k % 2) * PAIR_COLS
             copy(
-                out=grouped[u][:, g].rearrange("p (c i) t -> p c t i", i=4),
-                in_=raw_lo[(u, g)].rearrange("p t (c i) -> p c t i", i=4),
+                out=grouped[k][:, g, c0:c1].rearrange("p (c i) t -> p c t i", i=4),
+                in_=raw_lo[(k // 2, g)][:, :, first + c0 : first + c1].rearrange("p t (c i) -> p c t i", i=4),
             )
 
         def quantize(values, tag):
-            codes = flow.tile([P, PASSES * P], U32, tag=tag + "_codes", name=tag + "_codes", align_bytes=64)
-            scales = flow.tile([P, PASSES * P], U8, tag=tag + "_scales", name=tag + "_scales", align_bytes=64)
+            words = values.shape[1] // PACK
+            codes = flow.tile([P, words], U32, tag=tag + "_codes", name=tag + "_codes", align_bytes=64)
+            scales = flow.tile([P, words], U8, tag=tag + "_scales", name=tag + "_scales", align_bytes=64)
             nc.vector.quantize_mx(out=codes[:].bitcast(FP8X4), scales=scales[:], in_=values)
-            return codes, scales
+            return [(codes[:, s * P : (s + 1) * P], scales[:, s * P : (s + 1) * P]) for s in range(words // P)]
 
-        def quantize_lo(u):
-            lo_q[u] = quantize(grouped[u][:].rearrange("p g r t -> p (g r t)"), "lo")
+        def quantize_lo(k, g0, g1):
+            parts = quantize(grouped[k][:, g0:g1].rearrange("p g r t -> p (g r t)"), "lo")
+            for g in range(g0, g1):
+                for i in range(2):
+                    lo_q[(2 * k + i, g)] = parts[2 * (g - g0) + i]
 
-        def quantize_h(u):
-            h_q[u] = quantize(ht[u][:].rearrange("p g r u -> p (g r u)").bitcast(BF16), "h")
+        def quantize_h(u0, count):
+            parts = quantize(ht[u0][:].rearrange("p i g r u -> p (i g r u)").bitcast(BF16), "h")
+            for i in range(count):
+                for g in range(PASSES):
+                    h_q[(u0 + i, g)] = parts[PASSES * i + g]
 
         def product(acc, stationary, moving, moving_scales):
-            codes, scales = stationary
             for g in range(PASSES):
+                codes, scales = stationary[g]
                 nc.tensor.matmul_mx(
                     out=acc[:],
-                    lhsT=codes[:, g * P : (g + 1) * P].bitcast(FP8X4),
-                    lhsT_scale=scales[:, g * P : (g + 1) * P],
+                    lhsT=codes.bitcast(FP8X4),
+                    lhsT_scale=scales,
                     rhs=moving[g].bitcast(FP4X4),
                     rhs_scale=moving_scales[g],
                     start=(g == 0),
                     stop=(g == PASSES - 1),
                 )
 
-        def hankel(u):
+        def hankel(u, h):
             j = u // 4
-            hs[u] = flow.tile([P, PASSES, 2, P, 2], BF16, tag="hs", name="hs")
-            for h in range(2):
-                acc = bank("h%d" % (2 * (u % 2) + h), [P, BANK])
-                product(acc, lo_q[u], [c_words[(j, g, h)] for g in range(PASSES)], [c_scales(j, g, h) for g in range(PASSES)])
-                nc.vector.tensor_tensor(
-                    out=hs[u][:, h],
-                    in0=acc[:].rearrange("r (p u e) -> r u p e", u=2, e=2),
-                    in1=c_rows[j][:, h],
-                    op=MULT,
-                )
+            if h == 0:
+                hs[u] = flow.tile([P, PASSES, 2, P, 2], BF16, tag="hs", name="hs")
+            acc = bank("h%d" % (2 * (u % 2) + h), [P, BANK])
+            product(
+                acc,
+                [lo_q[(u, g)] for g in range(PASSES)],
+                [c_words[(j, g, h)] for g in range(PASSES)],
+                [c_scales[(j, g)][:, h * BANK : (h + 1) * BANK] for g in range(PASSES)],
+            )
+            return acc
 
-        def turn(u, copy):
+        def scale_columns(u, h, acc):
+            nc.vector.tensor_tensor(
+                out=hs[u][:, h],
+                in0=acc[:].rearrange("r (p u e) -> r u p e", u=2, e=2),
+                in1=c_rows[u // 4][:, h],
+                op=MULT,
+            )
+
+        def turn(u, place, copy):
             words = hs[u][:].rearrange("r g u p e -> r (g u p e)").bitcast(F32)
             turned = bank("t%d" % (u % 2), [P, 2 * PASSES, P])
             for i in range(2 * PASSES):
                 nc.tensor.transpose(turned[:, i, :], words[:, i * P : (i + 1) * P], ident[:])
-            ht[u] = flow.tile([P, PASSES, P, 2], F32, tag="ht", name="ht", align_bytes=64)
-            copy(out=ht[u][:], in_=turned[:].rearrange("p (g u) r -> p g r u", u=2))
+            copy(out=place, in_=turned[:].rearrange("p (g u) r -> p g r u", u=2))
 
-        def sketch(u, on_vector):
+        def turned_tile(u0, count):
+            ht[u0] = flow.tile([P, count, PASSES, P, 2], F32, tag="ht", name="ht", align_bytes=64)
+            return ht[u0]
+
+        def sketch(u, tag):
+            j = u // 4
+            y_acc[u] = bank(tag, [P, BANK])
+            product(y_acc[u], [h_q[(u, g)] for g in range(PASSES)], [e_words[(j, g)] for g in range(PASSES)], [e_scales[(j, g)] for g in range(PASSES)])
+
+        def finish(u, on_vector):
             j, i = divmod(u, 4)
-            acc = bank("y%d" % (u % 2), [P, BANK])
-            product(acc, h_q[u], [e_words[j][:, g, :] for g in range(PASSES)], [e_scale[:, PASSES * j + g, :] for g in range(PASSES)])
-            result = flow.tile([P, N], F32, tag="result", name="result")
+            result = keep.tile([P, N], F32, name="result_%d" % u)
             if on_vector:
-                nc.vector.tensor_scalar(out=result[:], in0=acc[:], scalar1=o_cols[:, u : u + 1], scalar2=None, op0=MULT)
+                nc.vector.tensor_scalar(out=result[:], in0=y_acc[u][:], scalar1=columns[:, u : u + 1], scalar2=None, op0=MULT)
             else:
-                nc.scalar.activation(out=result[:], in_=acc[:], func=COPY, scale=o_cols[:, u : u + 1])
+                nc.scalar.activation(out=result[:], in_=y_acc[u][:], func=COPY, scale=columns[:, u : u + 1])
             nc.sync.dma_start(out=out[j, i * P : (i + 1) * P, :], in_=result[:])
 
-        nc.scalar.activation(out=o_pad[0:TILES, :], in_=o_rows[:], func=COPY)
-        c_pairs = c_quads[:].rearrange("p m t -> p (m t)").bitcast(F32)
-        c_banks = []
-        for j, tag in enumerate(("t0", "t1", "y0", "y1")):
-            spread = bank(tag, [P, 2 * PASSES, P])
+        def spread_c(j, tag):
+            c_banks[j] = bank(tag, [P, 2 * PASSES, P])
             for i in range(2 * PASSES):
-                m = 2 * PASSES * j + i
-                nc.tensor.transpose(spread[:, i, :], c_pairs[:, m : m + 1].to_broadcast([P, P]), ident[:])
-            c_banks.append(spread)
-        o_bank = bank("h3", [P, P])
-        nc.tensor.transpose(o_bank[:], o_pad[:], ident[:])
-        o_cols = keep.tile([P, TILES], F32, name="o_cols")
-        c_rows = {}
+                m = TILES + 2 * PASSES * j + i
+                nc.tensor.transpose(c_banks[j][:, i, :], columns[:, m : m + 1].to_broadcast([P, P]), ident[:])
 
         def fetch_c(j):
-            words = keep.tile([P, 2 * PASSES * P], F32, name="c_rows_%d" % j)
-            nc.scalar.copy(out=words[:], in_=c_banks[j][:].rearrange("r i p -> r (i p)"))
-            c_rows[j] = words[:].bitcast(BF16).rearrange("r (g u p e) -> r g u p e", g=PASSES, u=2, e=2)
+            words = keep.tile([P, PASSES, 2, P], F32, name="c_rows_%d" % j)
+            nc.scalar.copy(out=words[:], in_=c_banks[j][:].rearrange("r (g a) (b u) -> r g u (a b)", g=PASSES, u=2))
+            c_rows[j] = words[:].rearrange("r g u p -> r (g u p)").bitcast(BF16).rearrange("r (g u p e) -> r g u p e", g=PASSES, u=2, e=2)
 
-        for g in range(PASSES):
-            interleave(0, g, nc.vector.tensor_copy)
-            interleave(1, g, nc.scalar.copy)
+        nc.scalar.activation(out=factors[0:TILES, :], in_=o_rows[:], func=COPY)
+        factor_bank = bank("h3", [P, P])
+        nc.tensor.transpose(factor_bank[:], factors[:], ident[:])
+        columns = keep.tile([P, 2 * TILES], F32, name="columns")
+
+        interleave(0, 0, 0, PAIR_COLS, nc.vector.tensor_copy)
+        interleave(1, 0, 0, PAIR_COLS, nc.scalar.copy)
+        nc.vector.tensor_copy(out=columns[:], in_=factor_bank[:, 0 : 2 * TILES])
+        quantize_lo(0, 0, 1)
+        spread_c(0, "t0")
+        spread_c(1, "t1")
+        interleave(0, 1, 0, HEAD_SCALAR_COLS, nc.scalar.copy)
+        interleave(0, 1, HEAD_SCALAR_COLS, PAIR_COLS, nc.vector.tensor_copy)
+        quantize_lo(0, 1, 2)
         fetch_c(0)
-        nc.scalar.copy(out=o_cols[:], in_=o_bank[:, 0:TILES])
-        quantize_lo(0)
-        quantize_lo(1)
-        interleave(2, 0, nc.vector.tensor_copy)
 
-        for k in range(PAIRS + 2):
-            if 2 <= k:
-                quantize_h(2 * k - 4)
-                quantize_h(2 * k - 3)
+        for k in range(PAIRS + 1):
             if k + 1 < PAIRS:
-                interleave(2 * k + 2, 1, nc.scalar.copy)
-                interleave(2 * k + 3, 0, nc.scalar.copy)
-                interleave(2 * k + 3, 1, nc.scalar.copy)
+                interleave(k + 1, 1, SCALAR_COLS, PAIR_COLS, nc.vector.tensor_copy)
+                if 1 <= k:
+                    interleave(k + 1, 0, 0, PAIR_COLS, nc.scalar.copy)
+                interleave(k + 1, 1, 0, SCALAR_COLS, nc.scalar.copy)
             if k == 0:
-                for j in range(1, G):
-                    fetch_c(j)
-            if k < PAIRS:
-                hankel(2 * k)
-                hankel(2 * k + 1)
-            if k + 1 < PAIRS:
-                quantize_lo(2 * k + 2)
-                quantize_lo(2 * k + 3)
-            if k + 2 < PAIRS:
-                interleave(2 * k + 4, 0, nc.vector.tensor_copy)
-            if 1 <= k <= PAIRS:
-                turn(2 * k - 2, nc.scalar.copy)
-                turn(2 * k - 1, nc.vector.tensor_copy if k == PAIRS else nc.scalar.copy)
+                fetch_c(1)
+            if 3 <= k:
+                finish(2 * k - 5, False)
             if 2 <= k:
-                sketch(2 * k - 4, False)
-                sketch(2 * k - 3, k == PAIRS + 1)
+                quantize_h(2 * k - 4, 2)
+            if k < PAIRS:
+                for u in (2 * k, 2 * k + 1):
+                    for h in range(2):
+                        acc = hankel(u, h)
+                        if (u, h) == (2 * k + 1, 1) and k + 1 < PAIRS:
+                            quantize_lo(k + 1, 0, PASSES)
+                        scale_columns(u, h, acc)
+            if k == 0:
+                spread_c(2, "y0")
+                spread_c(3, "y1")
+            if 1 <= k < PAIRS:
+                pair = turned_tile(2 * k - 2, 2)
+                for i in range(2):
+                    turn(2 * k - 2 + i, pair[:, i], nc.scalar.copy)
+            if k == 1:
+                fetch_c(2)
+                fetch_c(3)
+            if k == PAIRS:
+                for u in (TILES - 2, TILES - 1):
+                    turn(u, turned_tile(u, 1)[:, 0], nc.vector.tensor_copy)
+            if 2 <= k:
+                sketch(2 * k - 4, "y0")
+                sketch(2 * k - 3, "y1")
+                finish(2 * k - 4, False)
+
+        finish(TILES - 3, False)
+        for u in (TILES - 2, TILES - 1):
+            quantize_h(u, 1)
+        sketch(TILES - 2, "h0")
+        sketch(TILES - 1, "h1")
+        finish(TILES - 2, False)
+        finish(TILES - 1, True)

@@ -19,64 +19,68 @@ MULT = mybir.AluOpType.mult
 P = 128
 PACK = 4
 K_PASS = P * PACK
-PASSES = 2
+PASSES = K // K_PASS
 BANK = 512
-TILES = G * R // P
+BANKS = 8
+HALVES = Q // BANK
+TILES_PER_GROUP = R // P
+TILES = G * TILES_PER_GROUP
 PAIRS = TILES // 2
 PAIR_COLS = 2 * P
-SCALAR_COLS = 64
-HEAD_SCALAR_COLS = 80
+WORD_TILES = 2 * PASSES
+RUN = 4
+FLOW_BUFS = 6
+
+FIRST_SCALAR_COLS = 80
+SECOND_SCALAR_COLS = 64
+LOOP_SCALAR_COLS = 96
 
 
 def tile_scaled_hankel_sketch_s14_kernel(tc, lo, lc_words, lc_scales, o_inv, c_inv, om_words, om_scales, out):
     nc = tc.nc
     with ExitStack() as ctx:
         keep = ctx.enter_context(tc.tile_pool(name="keep", bufs=1))
-        flow = ctx.enter_context(tc.tile_pool(name="flow", bufs=4))
+        flow = ctx.enter_context(tc.tile_pool(name="flow", bufs=FLOW_BUFS))
         psum = ctx.enter_context(tc.psum_pool(name="psum", bufs=1))
         ctx.enter_context(tc.manual_schedule())
 
-        lc_w32, lc_s32 = lc_words.bitcast(I32), lc_scales.bitcast(I32)
-        om_w32, om_s32 = om_words.bitcast(I32), om_scales.bitcast(I32)
+        banks_taken = []
 
-        def bank(tag, shape):
+        def bank(shape):
+            tag = "bank%d" % (len(banks_taken) % BANKS)
+            banks_taken.append(tag)
             return psum.tile(shape, F32, tag=tag, name=tag)
 
-        def scale_plane(name, j0, j1, width):
-            plane = keep.tile([P, PASSES * (j1 - j0), width], U8, name=name, align_bytes=64)
-            nc.vector.memset(plane[:].bitcast(I32), 0)
-            return plane
-
+        lc_w32, lc_s32 = lc_words.bitcast(I32), lc_scales.bitcast(I32)
+        om_w32, om_s32 = om_words.bitcast(I32), om_scales.bitcast(I32)
         raw_lo, c_words, c_scales, e_words, e_scales = {}, {}, {}, {}, {}
 
-        def load_scales(plane, rows, j0, j1, found):
-            rows = rows[PASSES * j0 : PASSES * j1]
+        def zeroed_planes(name, groups, width):
+            planes = keep.tile([P, PASSES * groups, width], U8, name=name, align_bytes=64)
+            nc.vector.memset(planes[:].bitcast(I32), 0)
+            return planes
+
+        def load_scales(planes, rows, j0, j1, found):
             for quad in range(4):
                 nc.sync.dma_start(
-                    out=plane[32 * quad : 32 * quad + 4].bitcast(I32),
-                    in_=rows[:, 4 * quad : 4 * quad + 4, :].rearrange("g r n -> r g n"),
+                    out=planes[32 * quad : 32 * quad + 4].bitcast(I32),
+                    in_=rows[PASSES * j0 : PASSES * j1, 4 * quad : 4 * quad + 4, :].rearrange("g r n -> r g n"),
                 )
             for j in range(j0, j1):
                 for g in range(PASSES):
-                    found[(j, g)] = plane[:, PASSES * (j - j0) + g, :]
+                    found[(j, g)] = planes[:, PASSES * (j - j0) + g, :]
 
         def load_words(name, rows):
-            passes, unused, words = rows.shape
-            codes = keep.tile([P, passes, 4 * words], U8, name=name, align_bytes=64)
+            codes = keep.tile([P, rows.shape[0], 4 * rows.shape[2]], U8, name=name, align_bytes=64)
             nc.sync.dma_start(out=codes[:].bitcast(I32), in_=rows.rearrange("g p n -> p g n"))
             return codes
 
-        def load_lo(j, g):
-            raw = keep.tile([P, PACK, R], BF16, name="lo_%d_%d" % (j, g), align_bytes=64)
-            rows = lo[j, g * K_PASS : (g + 1) * K_PASS, :]
-            nc.sync.dma_start(out=raw[:], in_=rows.rearrange("(p t) r -> p t r", t=PACK))
-            raw_lo[(j, g)] = raw
-
         def load_c_words(j, h0, h1):
-            codes = load_words("c_words_%d_%d" % (j, h0), lc_w32[PASSES * j : PASSES * (j + 1), :, h0 * 256 : h1 * 256])
+            rows = lc_w32[PASSES * j : PASSES * (j + 1), :, h0 * BANK // 2 : h1 * BANK // 2]
+            codes = load_words("c_words_%d_%d" % (j, h0), rows)
             for g in range(PASSES):
                 for h in range(h0, h1):
-                    c_words[(j, g, h)] = codes[:, g, (h - h0) * 1024 : (h - h0 + 1) * 1024]
+                    c_words[(j, g, h)] = codes[:, g, (h - h0) * 2 * BANK : (h - h0 + 1) * 2 * BANK]
 
         def load_e_words(j0, j1):
             codes = load_words("e_words_%d" % j0, om_w32[PASSES * j0 : PASSES * j1])
@@ -84,39 +88,47 @@ def tile_scaled_hankel_sketch_s14_kernel(tc, lo, lc_words, lc_scales, o_inv, c_i
                 for g in range(PASSES):
                     e_words[(j, g)] = codes[:, PASSES * (j - j0) + g, :]
 
-        factors = keep.tile([P, P], F32, name="factors")
-        nc.gpsimd.memset(factors[:], 0.0)
-        c_plane0 = scale_plane("c_plane0", 0, 1, Q)
-        c_plane1 = scale_plane("c_plane1", 1, 2, Q)
-        e_plane0 = scale_plane("e_plane0", 0, 1, N)
-        c_plane2 = scale_plane("c_plane2", 2, G, Q)
-        e_plane1 = scale_plane("e_plane1", 1, G, N)
+        def load_lo(j):
+            for g in range(PASSES):
+                raw = keep.tile([P, PACK, R], BF16, name="lo_%d_%d" % (j, g), align_bytes=64)
+                rows = lo[j, g * K_PASS : (g + 1) * K_PASS, :]
+                nc.sync.dma_start(out=raw[:], in_=rows.rearrange("(p t) r -> p t r", t=PACK))
+                raw_lo[(j, g)] = raw
+
+        c_pad = keep.tile([P, P], F32, name="c_pad")
+        nc.gpsimd.memset(c_pad[:], 0.0)
+        o_pad = keep.tile([P, P], F32, name="o_pad")
+        nc.gpsimd.memset(o_pad[:], 0.0)
+        c_planes_0 = zeroed_planes("c_planes_0", 1, Q)
+        c_planes_1 = zeroed_planes("c_planes_1", 1, Q)
+        e_planes_0 = zeroed_planes("e_planes_0", 1, N)
+        c_planes_rest = zeroed_planes("c_planes_rest", G - 2, Q)
+        e_planes_rest = zeroed_planes("e_planes_rest", G - 1, N)
         ident = keep.tile([P, P], F32, name="ident")
         make_identity(nc, ident[:])
 
         o_rows = keep.tile([TILES, P], BF16, name="o_rows")
         nc.sync.dma_start(out=o_rows[:], in_=o_inv.rearrange("j (i p) -> (j i) p", p=P))
-        load_lo(0, 0)
-        nc.sync.dma_start(out=factors[TILES : 2 * TILES, :].bitcast(BF16), in_=c_inv.rearrange("j (m w) -> (j m) w", w=2 * P))
-        load_lo(0, 1)
-        load_scales(c_plane0, lc_s32, 0, 1, c_scales)
+        c_row_count = G * WORD_TILES
+        nc.sync.dma_start(
+            out=c_pad[0:c_row_count, :].bitcast(BF16), in_=c_inv.rearrange("j (m w) -> (j m) w", m=WORD_TILES)
+        )
+        load_lo(0)
+        load_scales(c_planes_0, lc_s32, 0, 1, c_scales)
         load_c_words(0, 0, 1)
-        load_c_words(0, 1, 2)
-        load_lo(1, 0)
-        load_lo(1, 1)
-        load_scales(c_plane1, lc_s32, 1, 2, c_scales)
-        load_c_words(1, 0, 2)
-        load_scales(e_plane0, om_s32, 0, 1, e_scales)
+        load_c_words(0, 1, HALVES)
+        load_lo(1)
+        load_scales(c_planes_1, lc_s32, 1, 2, c_scales)
+        load_c_words(1, 0, HALVES)
+        load_lo(2)
+        load_scales(e_planes_0, om_s32, 0, 1, e_scales)
         load_e_words(0, 1)
-        load_lo(2, 0)
-        load_lo(2, 1)
-        load_scales(c_plane2, lc_s32, 2, G, c_scales)
-        load_c_words(2, 0, 2)
-        load_scales(e_plane1, om_s32, 1, G, e_scales)
+        load_scales(c_planes_rest, lc_s32, 2, G, c_scales)
+        load_c_words(2, 0, HALVES)
+        load_lo(3)
+        load_scales(e_planes_rest, om_s32, 1, G, e_scales)
         load_e_words(1, 2)
-        load_lo(3, 0)
-        load_lo(3, 1)
-        load_c_words(3, 0, 2)
+        load_c_words(3, 0, HALVES)
         load_e_words(2, G)
 
         grouped, lo_q, hs, ht, h_q, y_acc, c_banks, c_rows = {}, {}, {}, {}, {}, {}, {}, {}
@@ -126,8 +138,8 @@ def tile_scaled_hankel_sketch_s14_kernel(tc, lo, lc_words, lc_scales, o_inv, c_i
                 grouped[k] = flow.tile([P, PASSES, PAIR_COLS, PACK], BF16, tag="grouped", name="grouped", align_bytes=64)
             first = (k % 2) * PAIR_COLS
             copy(
-                out=grouped[k][:, g, c0:c1].rearrange("p (c i) t -> p c t i", i=4),
-                in_=raw_lo[(k // 2, g)][:, :, first + c0 : first + c1].rearrange("p t (c i) -> p c t i", i=4),
+                out=grouped[k][:, g, c0:c1].rearrange("p (c i) t -> p c t i", i=RUN),
+                in_=raw_lo[(k // 2, g)][:, :, first + c0 : first + c1].rearrange("p t (c i) -> p c t i", i=RUN),
             )
 
         def quantize(values, tag):
@@ -143,9 +155,9 @@ def tile_scaled_hankel_sketch_s14_kernel(tc, lo, lc_words, lc_scales, o_inv, c_i
                 for i in range(2):
                     lo_q[(2 * k + i, g)] = parts[2 * (g - g0) + i]
 
-        def quantize_h(u0, count):
-            parts = quantize(ht[u0][:].rearrange("p i g r u -> p (i g r u)").bitcast(BF16), "h")
-            for i in range(count):
+        def quantize_h(u0):
+            parts = quantize(ht[u0][:].rearrange("p i g r w -> p (i g r w)").bitcast(BF16), "h")
+            for i in range(len(parts) // PASSES):
                 for g in range(PASSES):
                     h_q[(u0 + i, g)] = parts[PASSES * i + g]
 
@@ -153,7 +165,7 @@ def tile_scaled_hankel_sketch_s14_kernel(tc, lo, lc_words, lc_scales, o_inv, c_i
             for g in range(PASSES):
                 codes, scales = stationary[g]
                 nc.tensor.matmul_mx(
-                    out=acc[:],
+                    out=acc,
                     lhsT=codes.bitcast(FP8X4),
                     lhsT_scale=scales,
                     rhs=moving[g].bitcast(FP4X4),
@@ -163,119 +175,135 @@ def tile_scaled_hankel_sketch_s14_kernel(tc, lo, lc_words, lc_scales, o_inv, c_i
                 )
 
         def hankel(u, h):
-            j = u // 4
-            if h == 0:
-                hs[u] = flow.tile([P, PASSES, 2, P, 2], BF16, tag="hs", name="hs")
-            acc = bank("h%d" % (2 * (u % 2) + h), [P, BANK])
+            j = u // TILES_PER_GROUP
+            acc = bank([P, BANK])
             product(
-                acc,
+                acc[:],
                 [lo_q[(u, g)] for g in range(PASSES)],
                 [c_words[(j, g, h)] for g in range(PASSES)],
                 [c_scales[(j, g)][:, h * BANK : (h + 1) * BANK] for g in range(PASSES)],
             )
-            return acc
-
-        def scale_columns(u, h, acc):
+            if h == 0:
+                hs[u] = flow.tile([P, HALVES, 2, P, 2], BF16, tag="hs", name="hs")
             nc.vector.tensor_tensor(
                 out=hs[u][:, h],
-                in0=acc[:].rearrange("r (p u e) -> r u p e", u=2, e=2),
-                in1=c_rows[u // 4][:, h],
+                in0=acc[:].rearrange("r (p w e) -> r w p e", w=2, e=2),
+                in1=c_rows[j][:, h],
                 op=MULT,
             )
 
-        def turn(u, place, copy):
-            words = hs[u][:].rearrange("r g u p e -> r (g u p e)").bitcast(F32)
-            turned = bank("t%d" % (u % 2), [P, 2 * PASSES, P])
-            for i in range(2 * PASSES):
+        def turn(u, together, copy):
+            u0 = u - u % together
+            if u == u0:
+                tag = "ht_%d" % together
+                ht[u0] = flow.tile([P, together, PASSES, P, 2], F32, tag=tag, name=tag, align_bytes=64)
+            words = hs[u][:].rearrange("r g w p e -> r (g w p e)").bitcast(F32)
+            turned = bank([P, WORD_TILES, P])
+            for i in range(WORD_TILES):
                 nc.tensor.transpose(turned[:, i, :], words[:, i * P : (i + 1) * P], ident[:])
-            copy(out=place, in_=turned[:].rearrange("p (g u) r -> p g r u", u=2))
+            copy(out=ht[u0][:, u - u0], in_=turned[:].rearrange("p (g w) r -> p g r w", w=2))
 
-        def turned_tile(u0, count):
-            ht[u0] = flow.tile([P, count, PASSES, P, 2], F32, tag="ht", name="ht", align_bytes=64)
-            return ht[u0]
+        def sketch_columns(acc, u, n0, n1):
+            j = u // TILES_PER_GROUP
+            product(
+                acc,
+                [h_q[(u, g)] for g in range(PASSES)],
+                [e_words[(j, g)][:, 2 * n0 : 2 * n1] for g in range(PASSES)],
+                [e_scales[(j, g)][:, n0:n1] for g in range(PASSES)],
+            )
 
-        def sketch(u, tag):
-            j = u // 4
-            y_acc[u] = bank(tag, [P, BANK])
-            product(y_acc[u], [h_q[(u, g)] for g in range(PASSES)], [e_words[(j, g)] for g in range(PASSES)], [e_scales[(j, g)] for g in range(PASSES)])
+        def scale_rows_and_store(acc, u, n0, n1, on_vector):
+            j, i = divmod(u, TILES_PER_GROUP)
+            result = keep.tile([P, n1 - n0], F32, name="result_%d_%d" % (u, n0))
+            if on_vector:
+                nc.vector.tensor_scalar(out=result[:], in0=acc, scalar1=o_cols[:, u : u + 1], scalar2=None, op0=MULT)
+            else:
+                nc.scalar.activation(out=result[:], in_=acc, func=COPY, scale=o_cols[:, u : u + 1])
+            nc.sync.dma_start(out=out[j, i * P : (i + 1) * P, n0:n1], in_=result[:])
+
+        def sketch(u):
+            y_acc[u] = bank([P, N])
+            sketch_columns(y_acc[u][:], u, 0, N)
 
         def finish(u, on_vector):
-            j, i = divmod(u, 4)
-            result = keep.tile([P, N], F32, name="result_%d" % u)
-            if on_vector:
-                nc.vector.tensor_scalar(out=result[:], in0=y_acc[u][:], scalar1=columns[:, u : u + 1], scalar2=None, op0=MULT)
-            else:
-                nc.scalar.activation(out=result[:], in_=y_acc[u][:], func=COPY, scale=columns[:, u : u + 1])
-            nc.sync.dma_start(out=out[j, i * P : (i + 1) * P, :], in_=result[:])
+            scale_rows_and_store(y_acc[u][:], u, 0, N, on_vector)
 
-        def spread_c(j, tag):
-            c_banks[j] = bank(tag, [P, 2 * PASSES, P])
-            for i in range(2 * PASSES):
-                m = TILES + 2 * PASSES * j + i
-                nc.tensor.transpose(c_banks[j][:, i, :], columns[:, m : m + 1].to_broadcast([P, P]), ident[:])
+        def spread_c(j):
+            c_banks[j] = bank([P, WORD_TILES, P])
+            for i in range(WORD_TILES):
+                m = WORD_TILES * j + i
+                nc.tensor.transpose(c_banks[j][:, i, :], c_cols[:, m : m + 1].to_broadcast([P, P]), ident[:])
 
         def fetch_c(j):
-            words = keep.tile([P, PASSES, 2, P], F32, name="c_rows_%d" % j)
-            nc.scalar.copy(out=words[:], in_=c_banks[j][:].rearrange("r (g a) (b u) -> r g u (a b)", g=PASSES, u=2))
-            c_rows[j] = words[:].rearrange("r g u p -> r (g u p)").bitcast(BF16).rearrange("r (g u p e) -> r g u p e", g=PASSES, u=2, e=2)
+            words = keep.tile([P, HALVES, 2, P], F32, name="c_rows_%d" % j)
+            nc.scalar.copy(out=words[:], in_=c_banks[j][:].rearrange("r (h a) (b w) -> r h w (a b)", h=HALVES, w=2))
+            values = words[:].rearrange("r h w p -> r (h w p)").bitcast(BF16)
+            c_rows[j] = values.rearrange("r (h w p e) -> r h w p e", h=HALVES, w=2, e=2)
 
-        nc.scalar.activation(out=factors[0:TILES, :], in_=o_rows[:], func=COPY)
-        factor_bank = bank("h3", [P, P])
-        nc.tensor.transpose(factor_bank[:], factors[:], ident[:])
-        columns = keep.tile([P, 2 * TILES], F32, name="columns")
+        nc.scalar.activation(out=o_pad[0:TILES, :], in_=o_rows[:], func=COPY)
+        c_turned = bank([P, P])
+        nc.tensor.transpose(c_turned[:], c_pad[:], ident[:])
+        c_cols = keep.tile([P, c_row_count], F32, name="c_cols")
+        nc.scalar.copy(out=c_cols[:], in_=c_turned[:, 0:c_row_count])
+        for j in range(G):
+            spread_c(j)
+        o_turned = bank([P, P])
+        nc.tensor.transpose(o_turned[:], o_pad[:], ident[:])
 
         interleave(0, 0, 0, PAIR_COLS, nc.vector.tensor_copy)
         interleave(1, 0, 0, PAIR_COLS, nc.scalar.copy)
-        nc.vector.tensor_copy(out=columns[:], in_=factor_bank[:, 0 : 2 * TILES])
         quantize_lo(0, 0, 1)
-        spread_c(0, "t0")
-        spread_c(1, "t1")
-        interleave(0, 1, 0, HEAD_SCALAR_COLS, nc.scalar.copy)
-        interleave(0, 1, HEAD_SCALAR_COLS, PAIR_COLS, nc.vector.tensor_copy)
+        interleave(0, 1, 0, FIRST_SCALAR_COLS, nc.scalar.copy)
+        interleave(0, 1, FIRST_SCALAR_COLS, PAIR_COLS, nc.vector.tensor_copy)
         quantize_lo(0, 1, 2)
         fetch_c(0)
+        interleave(1, 1, SECOND_SCALAR_COLS, PAIR_COLS, nc.vector.tensor_copy)
+        interleave(1, 1, 0, SECOND_SCALAR_COLS, nc.scalar.copy)
+        quantize_lo(1, 0, PASSES)
+        for j in range(1, G):
+            fetch_c(j)
+        o_cols = keep.tile([P, TILES], F32, name="o_cols")
+        nc.scalar.copy(out=o_cols[:], in_=o_turned[:, 0:TILES])
 
-        for k in range(PAIRS + 1):
-            if k + 1 < PAIRS:
-                interleave(k + 1, 1, SCALAR_COLS, PAIR_COLS, nc.vector.tensor_copy)
-                if 1 <= k:
-                    interleave(k + 1, 0, 0, PAIR_COLS, nc.scalar.copy)
-                interleave(k + 1, 1, 0, SCALAR_COLS, nc.scalar.copy)
-            if k == 0:
-                fetch_c(1)
-            if 3 <= k:
-                finish(2 * k - 5, False)
-            if 2 <= k:
-                quantize_h(2 * k - 4, 2)
-            if k < PAIRS:
-                for u in (2 * k, 2 * k + 1):
-                    for h in range(2):
-                        acc = hankel(u, h)
-                        if (u, h) == (2 * k + 1, 1) and k + 1 < PAIRS:
-                            quantize_lo(k + 1, 0, PASSES)
-                        scale_columns(u, h, acc)
-            if k == 0:
-                spread_c(2, "y0")
-                spread_c(3, "y1")
-            if 1 <= k < PAIRS:
-                pair = turned_tile(2 * k - 2, 2)
-                for i in range(2):
-                    turn(2 * k - 2 + i, pair[:, i], nc.scalar.copy)
-            if k == 1:
-                fetch_c(2)
-                fetch_c(3)
-            if k == PAIRS:
-                for u in (TILES - 2, TILES - 1):
-                    turn(u, turned_tile(u, 1)[:, 0], nc.vector.tensor_copy)
-            if 2 <= k:
-                sketch(2 * k - 4, "y0")
-                sketch(2 * k - 3, "y1")
-                finish(2 * k - 4, False)
+        for k in range(PAIRS):
+            prepares_next = 1 <= k < PAIRS - 1
+            if prepares_next:
+                scalar_cols = PAIR_COLS if k == 1 else LOOP_SCALAR_COLS
+                if scalar_cols < PAIR_COLS:
+                    interleave(k + 1, 1, scalar_cols, PAIR_COLS, nc.vector.tensor_copy)
+                interleave(k + 1, 0, 0, PAIR_COLS, nc.scalar.copy)
+                interleave(k + 1, 1, 0, scalar_cols, nc.scalar.copy)
+            if k >= 3:
+                finish(2 * (k - 3) + 1, False)
+            if k >= 2:
+                quantize_h(2 * (k - 2))
+            banks_ahead = 2 if k == 1 else 3
+            for n in range(2 * HALVES):
+                if prepares_next and n == banks_ahead:
+                    quantize_lo(k + 1, 0, PASSES)
+                hankel(2 * k + n // HALVES, n % HALVES)
+            if prepares_next:
+                turn(2 * (k - 1), 2, nc.scalar.copy)
+                turn(2 * (k - 1) + 1, 2, nc.scalar.copy)
+                if k >= 2:
+                    sketch(2 * (k - 2))
+                    sketch(2 * (k - 2) + 1)
+                    finish(2 * (k - 2), False)
 
-        finish(TILES - 3, False)
-        for u in (TILES - 2, TILES - 1):
-            quantize_h(u, 1)
-        sketch(TILES - 2, "h0")
-        sketch(TILES - 1, "h1")
-        finish(TILES - 2, False)
-        finish(TILES - 1, True)
+        first = TILES - 4
+        turn(first, 1, nc.scalar.copy)
+        turn(first + 1, 1, nc.vector.tensor_copy)
+        quantize_h(first)
+        turn(first + 2, 1, nc.scalar.copy)
+        turn(first + 3, 1, nc.vector.tensor_copy)
+        for u in range(first + 1, TILES):
+            quantize_h(u)
+        for u in range(first - 2, TILES - 1):
+            sketch(u)
+            finish(u, u == TILES - 3)
+        last = TILES - 1
+        for n0, on_vector in ((0, True), (N // 2, False)):
+            acc = bank([P, N // 2])
+            for c0 in range(0, N // 2, P):
+                sketch_columns(acc[:, c0 : c0 + P], last, n0 + c0, n0 + c0 + P)
+            scale_rows_and_store(acc[:], last, n0, n0 + N // 2, on_vector)

@@ -1,4 +1,5 @@
 from contextlib import ExitStack
+from functools import partial
 
 import concourse.mybir as mybir
 from concourse.masks import make_identity
@@ -30,10 +31,10 @@ PAIR_COLS = 2 * P
 WORD_TILES = 2 * PASSES
 RUN = 4
 FLOW_BUFS = 6
+HS_BUFS = 8
 
 FIRST_SCALAR_COLS = 80
 SECOND_SCALAR_COLS = 64
-LOOP_SCALAR_COLS = 96
 
 
 def tile_scaled_hankel_sketch_s14_kernel(tc, lo, lc_words, lc_scales, o_inv, c_inv, om_words, om_scales, out):
@@ -184,13 +185,19 @@ def tile_scaled_hankel_sketch_s14_kernel(tc, lo, lc_words, lc_scales, o_inv, c_i
                 [c_scales[(j, g)][:, h * BANK : (h + 1) * BANK] for g in range(PASSES)],
             )
             if h == 0:
-                hs[u] = flow.tile([P, HALVES, 2, P, 2], BF16, tag="hs", name="hs")
+                hs[u] = flow.tile([P, HALVES, 2, P, 2], BF16, tag="hs", name="hs", bufs=HS_BUFS)
             nc.vector.tensor_tensor(
                 out=hs[u][:, h],
                 in0=acc[:].rearrange("r (p w e) -> r w p e", w=2, e=2),
                 in1=c_rows[j][:, h],
                 op=MULT,
             )
+
+        def hankel_pair(k, between):
+            for n in range(2 * HALVES):
+                if n in between:
+                    between[n]()
+                hankel(2 * k + n // HALVES, n % HALVES)
 
         def turn(u, together, copy):
             u0 = u - u % together
@@ -265,30 +272,32 @@ def tile_scaled_hankel_sketch_s14_kernel(tc, lo, lc_words, lc_scales, o_inv, c_i
         o_cols = keep.tile([P, TILES], F32, name="o_cols")
         nc.scalar.copy(out=o_cols[:], in_=o_turned[:, 0:TILES])
 
-        for k in range(PAIRS):
-            prepares_next = 1 <= k < PAIRS - 1
-            if prepares_next:
-                scalar_cols = PAIR_COLS if k == 1 else LOOP_SCALAR_COLS
-                if scalar_cols < PAIR_COLS:
-                    interleave(k + 1, 1, scalar_cols, PAIR_COLS, nc.vector.tensor_copy)
-                interleave(k + 1, 0, 0, PAIR_COLS, nc.scalar.copy)
-                interleave(k + 1, 1, 0, scalar_cols, nc.scalar.copy)
-            if k >= 3:
-                finish(2 * (k - 3) + 1, False)
-            if k >= 2:
-                quantize_h(2 * (k - 2))
-            banks_ahead = 2 if k == 1 else 3
-            for n in range(2 * HALVES):
-                if prepares_next and n == banks_ahead:
-                    quantize_lo(k + 1, 0, PASSES)
-                hankel(2 * k + n // HALVES, n % HALVES)
-            if prepares_next:
-                turn(2 * (k - 1), 2, nc.scalar.copy)
-                turn(2 * (k - 1) + 1, 2, nc.scalar.copy)
-                if k >= 2:
-                    sketch(2 * (k - 2))
-                    sketch(2 * (k - 2) + 1)
-                    finish(2 * (k - 2), False)
+        for k, g in ((2, 0), (2, 1), (3, 0), (3, 1), (4, 0)):
+            interleave(k, g, 0, PAIR_COLS, nc.scalar.copy)
+        hankel_pair(0, {})
+        hankel_pair(1, {1: partial(quantize_lo, 2, 0, PASSES)})
+
+        for j in range(1, G):
+            k = 2 * j
+            done = TILES_PER_GROUP * (j - 1)
+            more = j + 1 < G
+            hankel_pair(k, {2: partial(quantize_lo, k + 1, 0, PASSES)})
+            if more:
+                interleave(k + 2, 1, 0, PAIR_COLS, nc.vector.tensor_copy)
+            for u in range(done, done + TILES_PER_GROUP):
+                turn(u, 2, nc.scalar.copy)
+            quantize_h(done)
+            between = {1: partial(quantize_h, done + 2)}
+            if more:
+                for g in range(PASSES):
+                    interleave(k + 3, g, 0, PAIR_COLS, nc.scalar.copy)
+                if k + 4 < PAIRS:
+                    interleave(k + 4, 0, 0, PAIR_COLS, nc.scalar.copy)
+                between[2] = partial(quantize_lo, k + 2, 0, PASSES)
+            hankel_pair(k + 1, between)
+            for u in range(done, done + (TILES_PER_GROUP if more else 2)):
+                sketch(u)
+                finish(u, False)
 
         first = TILES - 4
         turn(first, 1, nc.scalar.copy)

from contextlib import ExitStack
from functools import partial

import concourse.mybir as mybir
from concourse.masks import make_identity

G, K, R, Q, N = 4, 1024, 512, 1024, 512
FLOPS = 2 * G * (K * R * Q + R * Q * N)

F32 = mybir.dt.float32
BF16 = mybir.dt.bfloat16
I32 = mybir.dt.int32
U32 = mybir.dt.uint32
U8 = mybir.dt.uint8
FP8X4 = mybir.dt.float8_e4m3fn_x4
FP4X4 = mybir.dt.float4_e2m1fn_x4
COPY = mybir.ActivationFunctionType.Copy
MULT = mybir.AluOpType.mult

P = 128
PACK = 4
K_PASS = P * PACK
PASSES = K // K_PASS
BANK = 512
BANKS = 8
HALVES = Q // BANK
TILES_PER_GROUP = R // P
TILES = G * TILES_PER_GROUP
PAIRS = TILES // 2
PAIR_COLS = 2 * P
WORD_TILES = 2 * PASSES
RUN = 4
FLOW_BUFS = 6
HS_BUFS = 8

FIRST_SCALAR_COLS = 80
SECOND_SCALAR_COLS = 64


def tile_scaled_hankel_sketch_s14_kernel(tc, lo, lc_words, lc_scales, o_inv, c_inv, om_words, om_scales, out):
    nc = tc.nc
    with ExitStack() as ctx:
        keep = ctx.enter_context(tc.tile_pool(name="keep", bufs=1))
        flow = ctx.enter_context(tc.tile_pool(name="flow", bufs=FLOW_BUFS))
        psum = ctx.enter_context(tc.psum_pool(name="psum", bufs=1))
        ctx.enter_context(tc.manual_schedule())

        banks_taken = []

        def bank(shape):
            tag = "bank%d" % (len(banks_taken) % BANKS)
            banks_taken.append(tag)
            return psum.tile(shape, F32, tag=tag, name=tag)

        lc_w32, lc_s32 = lc_words.bitcast(I32), lc_scales.bitcast(I32)
        om_w32, om_s32 = om_words.bitcast(I32), om_scales.bitcast(I32)
        raw_lo, c_words, c_scales, e_words, e_scales = {}, {}, {}, {}, {}

        def zeroed_planes(name, groups, width):
            planes = keep.tile([P, PASSES * groups, width], U8, name=name, align_bytes=64)
            nc.vector.memset(planes[:].bitcast(I32), 0)
            return planes

        def load_scales(planes, rows, j0, j1, found):
            for quad in range(4):
                nc.sync.dma_start(
                    out=planes[32 * quad : 32 * quad + 4].bitcast(I32),
                    in_=rows[PASSES * j0 : PASSES * j1, 4 * quad : 4 * quad + 4, :].rearrange("g r n -> r g n"),
                )
            for j in range(j0, j1):
                for g in range(PASSES):
                    found[(j, g)] = planes[:, PASSES * (j - j0) + g, :]

        def load_words(name, rows):
            codes = keep.tile([P, rows.shape[0], 4 * rows.shape[2]], U8, name=name, align_bytes=64)
            nc.sync.dma_start(out=codes[:].bitcast(I32), in_=rows.rearrange("g p n -> p g n"))
            return codes

        def load_c_words(j, h0, h1):
            rows = lc_w32[PASSES * j : PASSES * (j + 1), :, h0 * BANK // 2 : h1 * BANK // 2]
            codes = load_words("c_words_%d_%d" % (j, h0), rows)
            for g in range(PASSES):
                for h in range(h0, h1):
                    c_words[(j, g, h)] = codes[:, g, (h - h0) * 2 * BANK : (h - h0 + 1) * 2 * BANK]

        def load_e_words(j0, j1):
            codes = load_words("e_words_%d" % j0, om_w32[PASSES * j0 : PASSES * j1])
            for j in range(j0, j1):
                for g in range(PASSES):
                    e_words[(j, g)] = codes[:, PASSES * (j - j0) + g, :]

        def load_lo(j):
            for g in range(PASSES):
                raw = keep.tile([P, PACK, R], BF16, name="lo_%d_%d" % (j, g), align_bytes=64)
                rows = lo[j, g * K_PASS : (g + 1) * K_PASS, :]
                nc.sync.dma_start(out=raw[:], in_=rows.rearrange("(p t) r -> p t r", t=PACK))
                raw_lo[(j, g)] = raw

        c_pad = keep.tile([P, P], F32, name="c_pad")
        nc.gpsimd.memset(c_pad[:], 0.0)
        o_pad = keep.tile([P, P], F32, name="o_pad")
        nc.gpsimd.memset(o_pad[:], 0.0)
        c_planes_0 = zeroed_planes("c_planes_0", 1, Q)
        c_planes_1 = zeroed_planes("c_planes_1", 1, Q)
        e_planes_0 = zeroed_planes("e_planes_0", 1, N)
        c_planes_rest = zeroed_planes("c_planes_rest", G - 2, Q)
        e_planes_rest = zeroed_planes("e_planes_rest", G - 1, N)
        ident = keep.tile([P, P], F32, name="ident")
        make_identity(nc, ident[:])

        o_rows = keep.tile([TILES, P], BF16, name="o_rows")
        nc.sync.dma_start(out=o_rows[:], in_=o_inv.rearrange("j (i p) -> (j i) p", p=P))
        c_row_count = G * WORD_TILES
        nc.sync.dma_start(
            out=c_pad[0:c_row_count, :].bitcast(BF16), in_=c_inv.rearrange("j (m w) -> (j m) w", m=WORD_TILES)
        )
        load_lo(0)
        load_scales(c_planes_0, lc_s32, 0, 1, c_scales)
        load_c_words(0, 0, 1)
        load_c_words(0, 1, HALVES)
        load_lo(1)
        load_scales(c_planes_1, lc_s32, 1, 2, c_scales)
        load_c_words(1, 0, HALVES)
        load_lo(2)
        load_scales(e_planes_0, om_s32, 0, 1, e_scales)
        load_e_words(0, 1)
        load_scales(c_planes_rest, lc_s32, 2, G, c_scales)
        load_c_words(2, 0, HALVES)
        load_lo(3)
        load_scales(e_planes_rest, om_s32, 1, G, e_scales)
        load_e_words(1, 2)
        load_c_words(3, 0, HALVES)
        load_e_words(2, G)

        grouped, lo_q, hs, ht, h_q, y_acc, c_banks, c_rows = {}, {}, {}, {}, {}, {}, {}, {}

        def interleave(k, g, c0, c1, copy):
            if k not in grouped:
                grouped[k] = flow.tile([P, PASSES, PAIR_COLS, PACK], BF16, tag="grouped", name="grouped", align_bytes=64)
            first = (k % 2) * PAIR_COLS
            copy(
                out=grouped[k][:, g, c0:c1].rearrange("p (c i) t -> p c t i", i=RUN),
                in_=raw_lo[(k // 2, g)][:, :, first + c0 : first + c1].rearrange("p t (c i) -> p c t i", i=RUN),
            )

        def quantize(values, tag):
            words = values.shape[1] // PACK
            codes = flow.tile([P, words], U32, tag=tag + "_codes", name=tag + "_codes", align_bytes=64)
            scales = flow.tile([P, words], U8, tag=tag + "_scales", name=tag + "_scales", align_bytes=64)
            nc.vector.quantize_mx(out=codes[:].bitcast(FP8X4), scales=scales[:], in_=values)
            return [(codes[:, s * P : (s + 1) * P], scales[:, s * P : (s + 1) * P]) for s in range(words // P)]

        def quantize_lo(k, g0, g1):
            parts = quantize(grouped[k][:, g0:g1].rearrange("p g r t -> p (g r t)"), "lo")
            for g in range(g0, g1):
                for i in range(2):
                    lo_q[(2 * k + i, g)] = parts[2 * (g - g0) + i]

        def quantize_h(u0):
            parts = quantize(ht[u0][:].rearrange("p i g r w -> p (i g r w)").bitcast(BF16), "h")
            for i in range(len(parts) // PASSES):
                for g in range(PASSES):
                    h_q[(u0 + i, g)] = parts[PASSES * i + g]

        def product(acc, stationary, moving, moving_scales):
            for g in range(PASSES):
                codes, scales = stationary[g]
                nc.tensor.matmul_mx(
                    out=acc,
                    lhsT=codes.bitcast(FP8X4),
                    lhsT_scale=scales,
                    rhs=moving[g].bitcast(FP4X4),
                    rhs_scale=moving_scales[g],
                    start=(g == 0),
                    stop=(g == PASSES - 1),
                )

        def hankel(u, h):
            j = u // TILES_PER_GROUP
            acc = bank([P, BANK])
            product(
                acc[:],
                [lo_q[(u, g)] for g in range(PASSES)],
                [c_words[(j, g, h)] for g in range(PASSES)],
                [c_scales[(j, g)][:, h * BANK : (h + 1) * BANK] for g in range(PASSES)],
            )
            if h == 0:
                hs[u] = flow.tile([P, HALVES, 2, P, 2], BF16, tag="hs", name="hs", bufs=HS_BUFS)
            nc.vector.tensor_tensor(
                out=hs[u][:, h],
                in0=acc[:].rearrange("r (p w e) -> r w p e", w=2, e=2),
                in1=c_rows[j][:, h],
                op=MULT,
            )

        def hankel_pair(k, between):
            for n in range(2 * HALVES):
                if n in between:
                    between[n]()
                hankel(2 * k + n // HALVES, n % HALVES)

        def turn(u, together, copy):
            u0 = u - u % together
            if u == u0:
                tag = "ht_%d" % together
                ht[u0] = flow.tile([P, together, PASSES, P, 2], F32, tag=tag, name=tag, align_bytes=64)
            words = hs[u][:].rearrange("r g w p e -> r (g w p e)").bitcast(F32)
            turned = bank([P, WORD_TILES, P])
            for i in range(WORD_TILES):
                nc.tensor.transpose(turned[:, i, :], words[:, i * P : (i + 1) * P], ident[:])
            copy(out=ht[u0][:, u - u0], in_=turned[:].rearrange("p (g w) r -> p g r w", w=2))

        def sketch_columns(acc, u, n0, n1):
            j = u // TILES_PER_GROUP
            product(
                acc,
                [h_q[(u, g)] for g in range(PASSES)],
                [e_words[(j, g)][:, 2 * n0 : 2 * n1] for g in range(PASSES)],
                [e_scales[(j, g)][:, n0:n1] for g in range(PASSES)],
            )

        def scale_rows_and_store(acc, u, n0, n1, on_vector):
            j, i = divmod(u, TILES_PER_GROUP)
            result = keep.tile([P, n1 - n0], F32, name="result_%d_%d" % (u, n0))
            if on_vector:
                nc.vector.tensor_scalar(out=result[:], in0=acc, scalar1=o_cols[:, u : u + 1], scalar2=None, op0=MULT)
            else:
                nc.scalar.activation(out=result[:], in_=acc, func=COPY, scale=o_cols[:, u : u + 1])
            nc.sync.dma_start(out=out[j, i * P : (i + 1) * P, n0:n1], in_=result[:])

        def sketch(u):
            y_acc[u] = bank([P, N])
            sketch_columns(y_acc[u][:], u, 0, N)

        def finish(u, on_vector):
            scale_rows_and_store(y_acc[u][:], u, 0, N, on_vector)

        def spread_c(j):
            c_banks[j] = bank([P, WORD_TILES, P])
            for i in range(WORD_TILES):
                m = WORD_TILES * j + i
                nc.tensor.transpose(c_banks[j][:, i, :], c_cols[:, m : m + 1].to_broadcast([P, P]), ident[:])

        def fetch_c(j):
            words = keep.tile([P, HALVES, 2, P], F32, name="c_rows_%d" % j)
            nc.scalar.copy(out=words[:], in_=c_banks[j][:].rearrange("r (h a) (b w) -> r h w (a b)", h=HALVES, w=2))
            values = words[:].rearrange("r h w p -> r (h w p)").bitcast(BF16)
            c_rows[j] = values.rearrange("r (h w p e) -> r h w p e", h=HALVES, w=2, e=2)

        nc.scalar.activation(out=o_pad[0:TILES, :], in_=o_rows[:], func=COPY)
        c_turned = bank([P, P])
        nc.tensor.transpose(c_turned[:], c_pad[:], ident[:])
        c_cols = keep.tile([P, c_row_count], F32, name="c_cols")
        nc.scalar.copy(out=c_cols[:], in_=c_turned[:, 0:c_row_count])
        for j in range(G):
            spread_c(j)
        o_turned = bank([P, P])
        nc.tensor.transpose(o_turned[:], o_pad[:], ident[:])

        interleave(0, 0, 0, PAIR_COLS, nc.vector.tensor_copy)
        interleave(1, 0, 0, PAIR_COLS, nc.scalar.copy)
        quantize_lo(0, 0, 1)
        interleave(0, 1, 0, FIRST_SCALAR_COLS, nc.scalar.copy)
        interleave(0, 1, FIRST_SCALAR_COLS, PAIR_COLS, nc.vector.tensor_copy)
        quantize_lo(0, 1, 2)
        fetch_c(0)
        interleave(1, 1, SECOND_SCALAR_COLS, PAIR_COLS, nc.vector.tensor_copy)
        interleave(1, 1, 0, SECOND_SCALAR_COLS, nc.scalar.copy)
        quantize_lo(1, 0, PASSES)
        for j in range(1, G):
            fetch_c(j)
        o_cols = keep.tile([P, TILES], F32, name="o_cols")
        nc.scalar.copy(out=o_cols[:], in_=o_turned[:, 0:TILES])

        for k, g in ((2, 0), (2, 1), (3, 0), (3, 1), (4, 0)):
            interleave(k, g, 0, PAIR_COLS, nc.scalar.copy)
        hankel_pair(0, {})
        hankel_pair(1, {1: partial(quantize_lo, 2, 0, PASSES)})

        for j in range(1, G):
            k = 2 * j
            done = TILES_PER_GROUP * (j - 1)
            more = j + 1 < G
            hankel_pair(k, {2: partial(quantize_lo, k + 1, 0, PASSES)})
            if more:
                interleave(k + 2, 1, 0, PAIR_COLS, nc.vector.tensor_copy)
            for u in range(done, done + TILES_PER_GROUP):
                turn(u, 2, nc.scalar.copy)
            quantize_h(done)
            between = {1: partial(quantize_h, done + 2)}
            if more:
                for g in range(PASSES):
                    interleave(k + 3, g, 0, PAIR_COLS, nc.scalar.copy)
                if k + 4 < PAIRS:
                    interleave(k + 4, 0, 0, PAIR_COLS, nc.scalar.copy)
                between[2] = partial(quantize_lo, k + 2, 0, PASSES)
            hankel_pair(k + 1, between)
            for u in range(done, done + (TILES_PER_GROUP if more else 2)):
                sketch(u)
                finish(u, False)

        first = TILES - 4
        turn(first, 1, nc.scalar.copy)
        turn(first + 1, 1, nc.vector.tensor_copy)
        quantize_h(first)
        turn(first + 2, 1, nc.scalar.copy)
        turn(first + 3, 1, nc.vector.tensor_copy)
        for u in range(first + 1, TILES):
            quantize_h(u)
        for u in range(first - 2, TILES - 1):
            sketch(u)
            finish(u, u == TILES - 3)
        last = TILES - 1
        for n0, on_vector in ((0, True), (N // 2, False)):
            acc = bank([P, N // 2])
            for c0 in range(0, N // 2, P):
                sketch_columns(acc[:, c0 : c0 + P], last, n0 + c0, n0 + c0 + P)
            scale_rows_and_store(acc[:], last, n0, n0 + N // 2, on_vector)
